import numpy as np
import ml_dtypes


def mxq(x, axis, fmt="e4m3"):
    dtype, down = {"e4m3": (ml_dtypes.float8_e4m3fn, 7), "e5m2": (ml_dtypes.float8_e5m2, 14)}[fmt]
    v = np.moveaxis(np.asarray(x, np.float32).astype(ml_dtypes.bfloat16).astype(np.float64), axis, -1)
    blocks = v.reshape(v.shape[:-1] + (-1, 32))
    amax = np.abs(blocks).max(-1, keepdims=True)
    byte = np.maximum(np.where(amax > 0, np.frexp(amax)[1] - 1 + 127, 0) - down, 1)
    scale = np.exp2(byte - 127.0)
    codes = (blocks / scale).astype(np.float32).astype(dtype).astype(np.float64)
    return np.moveaxis((codes * scale).reshape(v.shape), -1, axis)


WIDE = False


def mx_kscale(k):
    if not WIDE:
        return np.ones(k)
    levels = np.array([30, -30])
    if k % 512:
        return np.exp2(np.random.permutation(np.resize(levels, k // 32))).repeat(32)
    a = np.empty((k // 512, 16))
    for p in range(k // 512):
        a[p, :8] = np.random.permutation(np.resize(levels, 8))
        for g in range(8):
            far = levels[np.abs(levels - a[p, g]) >= 10]
            a[p, g + 8] = far[np.random.randint(len(far))]
    return np.exp2(a.ravel()).repeat(32)


def f64(x):
    return np.asarray(x).astype(np.float64)


def striped(idx):
    return np.tile(np.asarray(idx).reshape(-1, 16).T, (8, 1)).astype(np.uint16)


def unstriped(offs):
    return offs[:16].T.reshape(-1).astype(np.int64)


E2M1 = np.array([0.0, 0.5, 1.0, 1.5, 2.0, 3.0, 4.0, 6.0, -0.0, -0.5, -1.0, -1.5, -2.0, -3.0, -4.0, -6.0])


def pack_weight(w, fmt):
    k, n = w.shape
    w = f64(np.asarray(w, np.float32).astype(ml_dtypes.bfloat16)).reshape(k // 32, 32, n)
    amax = np.abs(w).max(1)
    if fmt in ("e4m3", "e5m2"):
        byte = np.frexp(amax)[1] - 1 + 127 - (7 if fmt == "e4m3" else 14)
    else:
        mant, ex = np.frexp(amax / 6.0)
        byte = np.where(mant > 0.5, ex, ex - 1) + 127
    byte = np.clip(np.where(amax > 0, byte, 1), 1, 254)
    scaled = (w * np.exp2(127.0 - byte)[:, None, :]).reshape(k, n).astype(np.float32)
    by_word = np.ascontiguousarray(scaled.reshape(k // 512, 128, 4, n).transpose(0, 1, 3, 2))
    if fmt in ("e4m3", "e5m2"):
        words = by_word.astype(ml_dtypes.float8_e4m3fn if fmt == "e4m3" else ml_dtypes.float8_e5m2).view(np.uint8)
    else:
        c = by_word.astype(ml_dtypes.float4_e2m1fn).view(np.uint8) & 0xF
        words = (c[..., 0::2] | (c[..., 1::2] << 4)).reshape(k // 512, 128, 2 * n)
    return np.ascontiguousarray(words), np.ascontiguousarray(byte.astype(np.uint8).reshape(k // 512, 16, n))


def unpack_weight(words, scales, fmt):
    g, _, n = scales.shape
    words = np.ascontiguousarray(words).reshape(g, 128, n, -1)
    if fmt in ("e4m3", "e5m2"):
        vals = words.view(ml_dtypes.float8_e4m3fn if fmt == "e4m3" else ml_dtypes.float8_e5m2).astype(np.float64)
    else:
        nib = np.empty((g, 128, n, 4), np.uint8)
        nib[..., 0::2] = words & 0xF
        nib[..., 1::2] = words >> 4
        vals = E2M1[nib]
    vals = vals * np.repeat(np.exp2(scales.astype(np.float64) - 127.0), 8, axis=1)[..., None]
    return vals.transpose(0, 1, 3, 2).reshape(g * 512, n)


K, T, J, N, S, L = 1024, 1024, 256, 256, 512, 512


def setup_inputs():
    n = np.random.standard_normal
    idx = np.random.permutation(T)[:J]
    idx2 = np.random.permutation(S)[:J]
    fk = mx_kscale(K)
    fl = mx_kscale(L)
    xtp = pack_weight(n((K, T)) * np.random.uniform(0.4, 1.6, (1, T)) / fk[:, None], "e5m2")
    wap = pack_weight(n((K, N)) * 1 / np.sqrt(K) * fk[:, None], "e5m2")
    wbp = pack_weight(n((L, N)) * 1 / np.sqrt(L) * fl[:, None], "e4m3")
    return {
        "xt_words": xtp[0],
        "xt_scales": xtp[1],
        "wa_words": wap[0],
        "wa_scales": wap[1],
        "xs": (n((L, S)) * np.random.uniform(0.4, 1.6, (1, S)) / fl[:, None]).astype(np.float32),
        "wb_words": wbp[0],
        "wb_scales": wbp[1],
        "bi": (np.random.uniform(-0.6, 0.6, (1, N))).astype(np.float32),
        "rs": (1.0 * n((J, N))).astype(np.float32),
        "offs": striped(idx),
        "offs2": striped(idx2),
    }


def reference(xt_words, xt_scales, wa_words, wa_scales, xs, wb_words, wb_scales, bi, rs, offs, offs2):
    idx = unstriped(offs)
    idx2 = unstriped(offs2)
    xtu = unpack_weight(xt_words, xt_scales, "e5m2")
    wau = unpack_weight(wa_words, wa_scales, "e5m2")
    wbu = unpack_weight(wb_words, wb_scales, "e4m3")
    xtidxg = xtu[:, idx]
    a = xtidxg.T @ wau
    xsidx2q = mxq(f64(xs)[:, idx2], 0, "e5m2")
    b0 = xsidx2q.T @ wbu
    b2 = b0 + f64(bi)
    d = a - b2
    y = d / (np.max(np.abs(d), axis=1, keepdims=True) + 0.2) + 0.3 * f64(rs)
    return y

@@ -1,0 +1,137 @@
+from contextlib import ExitStack
+
+import concourse.mybir as mybir
+
+K, T, J, N, S, L = 1024, 1024, 256, 256, 512, 512
+FLOPS = 2 * J * N * (K + L)
+
+F32 = mybir.dt.float32
+BF16 = mybir.dt.bfloat16
+I32 = mybir.dt.int32
+U32 = mybir.dt.uint32
+U16 = mybir.dt.uint16
+U8 = mybir.dt.uint8
+E5M2X4 = mybir.dt.float8_e5m2_x4
+E4M3X4 = mybir.dt.float8_e4m3fn_x4
+ALU = mybir.AluOpType
+ACT = mybir.ActivationFunctionType
+COPY = ACT.Copy
+
+P = 128
+PACK = 4
+PASSES = K // (P * PACK)
+TILES = J // P
+
+
+def load_scale_rows(queue, plane, scales):
+    rows = scales.bitcast(I32).rearrange("z (q r) c -> r q z c", r=4)
+    for r in range(4):
+        queue.dma_start(out=plane[r:P:32, :, :].bitcast(I32), in_=rows[r])
+
+
+def words_of(packed, z):
+    return packed[z].rearrange("p c r -> p (c r)").bitcast(I32)
+
+
+def tile_list_rows_othertable_gapoverpeak_kernel(
+    tc, xt_words, xt_scales, wa_words, wa_scales, xs, wb_words, wb_scales, bi, rs, offs, offs2, out
+):
+    nc = tc.nc
+    with ExitStack() as ctx:
+        sb = ctx.enter_context(tc.tile_pool(name="sb", bufs=1))
+        ps = ctx.enter_context(tc.psum_pool(name="ps", bufs=1))
+
+        idx = sb.tile([P, J // 16], U16, name="idx")
+        idx2 = sb.tile([P, J // 16], U16, name="idx2")
+        xt_sc = sb.tile([P, PASSES, T], U8, name="xt_sc", tag="reused", align_bytes=64)
+        wa_sc = sb.tile([P, PASSES, N], U8, name="wa_sc", align_bytes=64)
+        wb_sc = sb.tile([P, 1, N], U8, name="wb_sc", align_bytes=64)
+        xs_pl = [sb.tile([P, 2, S], F32, name=f"xs_pl{u}", align_bytes=64) for u in range(2)]
+        xt_w = [sb.tile([P, T], U32, name=f"xt_w{z}", align_bytes=64) for z in range(PASSES)]
+        wa_w = sb.tile([P, PASSES, N], U32, name="wa_w", align_bytes=64)
+        wb_w = sb.tile([P, N], U32, name="wb_w", align_bytes=64)
+        bcol = sb.tile([P, 2], F32, name="bcol")
+        res = sb.tile([P, TILES, N], F32, name="res")
+        ramp = sb.tile([P, P], F32, name="ramp")
+        dist = sb.tile([P, P], F32, name="dist")
+        ident = sb.tile([P, P], F32, name="ident")
+
+        nc.vector.memset(xt_sc[:].rearrange("p z c -> p (z c)").bitcast(I32), 0)
+        nc.vector.memset(wa_sc[:].rearrange("p z c -> p (z c)").bitcast(I32), 0)
+        nc.gpsimd.iota(ramp[:], pattern=[[1, P]], base=0, channel_multiplier=-1, allow_small_or_imprecise_dtypes=True)
+        nc.gpsimd.memset(wb_sc[:].rearrange("p z c -> p (z c)").bitcast(I32), 0)
+        load_scale_rows(nc.gpsimd, wb_sc, wb_scales)
+
+        planes = xs.rearrange("(p u t) s -> u p t s", u=2, t=2)
+        for u in range(2):
+            nc.scalar.dma_start(out=xs_pl[u][:], in_=planes[u])
+        nc.scalar.dma_start(out=xt_w[0][:].bitcast(I32), in_=words_of(xt_words, 0))
+        nc.scalar.activation(dist[:], ramp[:], ACT.Abs)
+        nc.scalar.activation(ident[:], dist[:], ACT.Relu, bias=1.0, scale=-1.0)
+
+        nc.sync.dma_start(idx2[:], offs2)
+        nc.sync.dma_start(idx[:], offs)
+        load_scale_rows(nc.sync, xt_sc, xt_scales)
+        nc.sync.dma_start(out=wb_w[:].bitcast(I32), in_=words_of(wb_words, 0))
+        nc.sync.dma_start(out=bcol[:], in_=bi.rearrange("o (p c) -> p (o c)", c=2))
+        nc.sync.dma_start(out=xt_w[1][:].bitcast(I32), in_=words_of(xt_words, 1))
+        load_scale_rows(nc.sync, wa_sc, wa_scales)
+        nc.sync.dma_start(out=wa_w[:].bitcast(I32), in_=wa_words.rearrange("z p c r -> p z (c r)").bitcast(I32))
+        nc.sync.dma_start(out=res[:], in_=rs.rearrange("(h p) n -> p h n", p=P))
+
+        xt_gs = sb.tile([P, PASSES, J], U8, name="xt_gs", align_bytes=64)
+        for z in range(PASSES):
+            nc.vector.tensor_copy(xt_gs[:, z, :], xt_sc[:, z, :].indirect(idx[:]))
+
+        picked = sb.tile([P, PACK, J], F32, name="picked", align_bytes=64)
+        for t in range(PACK):
+            nc.scalar.activation(picked[:, t, :], xs_pl[t // 2][:, t % 2, :].indirect(idx2[:]), COPY)
+        woven = sb.tile([P, J, PACK], BF16, name="woven", tag="reused", align_bytes=64)
+        nc.vector.tensor_scalar(woven[:], picked[:].rearrange("p t c -> p c t"), -1.0, None, ALU.mult)
+        xs_q = sb.tile([P, J], U32, name="xs_q", align_bytes=64)
+        xs_qs = sb.tile([P, J], U8, name="xs_qs", align_bytes=64)
+        nc.vector.quantize_mx(out=xs_q[:].bitcast(E5M2X4), scales=xs_qs[:], in_=woven[:].rearrange("p c t -> p (c t)"))
+
+        xt_g = [sb.tile([P, J], U32, name=f"xt_g{z}", align_bytes=64) for z in range(PASSES)]
+        for z in range(PASSES):
+            nc.vector.tensor_copy(xt_g[z][:], xt_w[z][:].indirect(idx[:]))
+
+        bias_ps = ps.tile([P, 2, P], F32, name="bias_ps")
+        for c in range(2):
+            nc.tensor.transpose(bias_ps[:, c, :], bcol[:, c : c + 1].to_broadcast([P, P]), ident[:])
+        bias = sb.tile([P, P, 2], F32, name="bias")
+        nc.scalar.copy(bias[:], bias_ps[:].rearrange("p c m -> p m c"))
+
+        acc = [ps.tile([P, N], F32, name=f"acc{h}") for h in range(TILES)]
+        for h in range(TILES):
+            cols = slice(h * P, (h + 1) * P)
+            nc.tensor.matmul_mx(
+                out=acc[h][:], lhsT=xs_q[:, cols].bitcast(E5M2X4), lhsT_scale=xs_qs[:, cols],
+                rhs=wb_w[:].bitcast(E4M3X4), rhs_scale=wb_sc[:, 0, :], start=True, stop=False,
+            )
+        for h in range(TILES):
+            cols = slice(h * P, (h + 1) * P)
+            for z in range(PASSES):
+                nc.tensor.matmul_mx(
+                    out=acc[h][:], lhsT=xt_g[z][:, cols].bitcast(E5M2X4), lhsT_scale=xt_gs[:, z, cols],
+                    rhs=wa_w[:, z, :].bitcast(E5M2X4), rhs_scale=wa_sc[:, z, :], start=False, stop=(z == PASSES - 1),
+                )
+
+        res3 = sb.tile([P, TILES, N], F32, name="res3")
+        nc.scalar.activation(res3[:], res[:], COPY, scale=0.3)
+
+        gap = [sb.tile([P, N], F32, name=f"gap{h}") for h in range(TILES)]
+        peak = sb.tile([P, TILES], F32, name="peak")
+        den = sb.tile([P, TILES], F32, name="den")
+        inv = sb.tile([P, TILES], F32, name="inv")
+        for h in range(TILES):
+            nc.vector.tensor_tensor(gap[h][:], acc[h][:], bias[:].rearrange("p m c -> p (m c)"), ALU.subtract)
+        for h in range(TILES):
+            nc.vector.tensor_reduce(peak[:, h : h + 1], gap[h][:], mybir.AxisListType.X, ALU.max, apply_absolute_value=True)
+        nc.vector.tensor_scalar(den[:], peak[:], 0.2, None, ALU.add)
+        nc.vector.reciprocal(inv[:], den[:])
+        stores = (nc.sync, nc.scalar)
+        for h in range(TILES):
+            y = sb.tile([P, N], F32, name=f"y{h}")
+            nc.vector.scalar_tensor_tensor(y[:], gap[h][:], inv[:, h : h + 1], res3[:, h, :], ALU.mult, ALU.add)
+            stores[h].dma_start(out=out[h * P : (h + 1) * P, :], in_=y[:])

@@ -50,15 +50,11 @@ def tile_list_rows_othertable_gapoverpeak_kernel(
         xt_w = [sb.tile([P, T], U32, name=f"xt_w{z}", align_bytes=64) for z in range(PASSES)]
         wa_w = sb.tile([P, PASSES, N], U32, name="wa_w", align_bytes=64)
         wb_w = sb.tile([P, N], U32, name="wb_w", align_bytes=64)
-        bcol = sb.tile([P, 2], F32, name="bcol")
+        bcol = sb.tile([P, 8], F32, name="bcol")
         res = sb.tile([P, TILES, N], F32, name="res")
-        ramp = sb.tile([P, P], F32, name="ramp")
-        dist = sb.tile([P, P], F32, name="dist")
-        ident = sb.tile([P, P], F32, name="ident")
 
         nc.vector.memset(xt_sc[:].rearrange("p z c -> p (z c)").bitcast(I32), 0)
         nc.vector.memset(wa_sc[:].rearrange("p z c -> p (z c)").bitcast(I32), 0)
-        nc.gpsimd.iota(ramp[:], pattern=[[1, P]], base=0, channel_multiplier=-1, allow_small_or_imprecise_dtypes=True)
         nc.gpsimd.memset(wb_sc[:].rearrange("p z c -> p (z c)").bitcast(I32), 0)
         load_scale_rows(nc.gpsimd, wb_sc, wb_scales)
 
@@ -66,22 +62,25 @@ def tile_list_rows_othertable_gapoverpeak_kernel(
         for u in range(2):
             nc.scalar.dma_start(out=xs_pl[u][:], in_=planes[u])
         nc.scalar.dma_start(out=xt_w[0][:].bitcast(I32), in_=words_of(xt_words, 0))
-        nc.scalar.activation(dist[:], ramp[:], ACT.Abs)
-        nc.scalar.activation(ident[:], dist[:], ACT.Relu, bias=1.0, scale=-1.0)
 
         nc.sync.dma_start(idx2[:], offs2)
         nc.sync.dma_start(idx[:], offs)
         load_scale_rows(nc.sync, xt_sc, xt_scales)
         nc.sync.dma_start(out=wb_w[:].bitcast(I32), in_=words_of(wb_words, 0))
-        nc.sync.dma_start(out=bcol[:], in_=bi.rearrange("o (p c) -> p (o c)", c=2))
+        nc.sync.dma_start(out=bcol[:], in_=bi.rearrange("o (j c) -> o j c", c=8).broadcast_to([4, 32, 8]))
         nc.sync.dma_start(out=xt_w[1][:].bitcast(I32), in_=words_of(xt_words, 1))
-        load_scale_rows(nc.sync, wa_sc, wa_scales)
         nc.sync.dma_start(out=wa_w[:].bitcast(I32), in_=wa_words.rearrange("z p c r -> p z (c r)").bitcast(I32))
+        load_scale_rows(nc.sync, wa_sc, wa_scales)
         nc.sync.dma_start(out=res[:], in_=rs.rearrange("(h p) n -> p h n", p=P))
 
         xt_gs = sb.tile([P, PASSES, J], U8, name="xt_gs", align_bytes=64)
         for z in range(PASSES):
             nc.vector.tensor_copy(xt_gs[:, z, :], xt_sc[:, z, :].indirect(idx[:]))
+
+        spread = sb.tile([P, 8, 32], F32, name="spread", align_bytes=64)
+        turned = sb.tile([P, 8, 32], F32, name="turned", align_bytes=64)
+        nc.vector.tensor_copy(spread[:], bcol[:].unsqueeze(2).broadcast_to([P, 8, 32]))
+        nc.vector.transpose(turned[:].rearrange("p c j -> p (c j)"), spread[:].rearrange("p c j -> p (c j)"))
 
         picked = sb.tile([P, PACK, J], F32, name="picked", align_bytes=64)
         for t in range(PACK):
@@ -96,11 +95,8 @@ def tile_list_rows_othertable_gapoverpeak_kernel(
         for z in range(PASSES):
             nc.vector.tensor_copy(xt_g[z][:], xt_w[z][:].indirect(idx[:]))
 
-        bias_ps = ps.tile([P, 2, P], F32, name="bias_ps")
-        for c in range(2):
-            nc.tensor.transpose(bias_ps[:, c, :], bcol[:, c : c + 1].to_broadcast([P, P]), ident[:])
-        bias = sb.tile([P, P, 2], F32, name="bias")
-        nc.scalar.copy(bias[:], bias_ps[:].rearrange("p c m -> p m c"))
+        bias = sb.tile([P, 32, 8], F32, name="bias")
+        nc.scalar.copy(bias[:], turned[:].rearrange("p c j -> p j c"))
 
         acc = [ps.tile([P, N], F32, name=f"acc{h}") for h in range(TILES)]
         for h in range(TILES):
@@ -125,7 +121,7 @@ def tile_list_rows_othertable_gapoverpeak_kernel(
         den = sb.tile([P, TILES], F32, name="den")
         inv = sb.tile([P, TILES], F32, name="inv")
         for h in range(TILES):
-            nc.vector.tensor_tensor(gap[h][:], acc[h][:], bias[:].rearrange("p m c -> p (m c)"), ALU.subtract)
+            nc.vector.tensor_tensor(gap[h][:], acc[h][:], bias[:].rearrange("p j c -> p (j c)"), ALU.subtract)
         for h in range(TILES):
             nc.vector.tensor_reduce(peak[:, h : h + 1], gap[h][:], mybir.AxisListType.X, ALU.max, apply_absolute_value=True)
         nc.vector.tensor_scalar(den[:], peak[:], 0.2, None, ALU.add)

@@ -43,31 +43,41 @@ def tile_list_rows_othertable_gapoverpeak_kernel(
 
         idx = sb.tile([P, J // 16], U16, name="idx")
         idx2 = sb.tile([P, J // 16], U16, name="idx2")
-        xt_sc = sb.tile([P, PASSES, T], U8, name="xt_sc", tag="reused", align_bytes=64)
+        xt_sc = sb.tile([P, PASSES, T], U8, name="xt_sc", align_bytes=64)
         wa_sc = sb.tile([P, PASSES, N], U8, name="wa_sc", align_bytes=64)
         wb_sc = sb.tile([P, 1, N], U8, name="wb_sc", align_bytes=64)
-        xs_pl = [sb.tile([P, 2, S], F32, name=f"xs_pl{u}", align_bytes=64) for u in range(2)]
+        xs_pl = [sb.tile([P, 2, S], F32, name=f"xs_pl{u}", tag=f"xs_pl{u}", align_bytes=64) for u in range(2)]
         xt_w = [sb.tile([P, T], U32, name=f"xt_w{z}", align_bytes=64) for z in range(PASSES)]
         wa_w = sb.tile([P, PASSES, N], U32, name="wa_w", align_bytes=64)
         wb_w = sb.tile([P, N], U32, name="wb_w", align_bytes=64)
-        bcol = sb.tile([P, 8], F32, name="bcol")
+        bcol = sb.tile([P, 2], F32, name="bcol")
         res = sb.tile([P, TILES, N], F32, name="res")
+        ident = sb.tile([P, P], F32, name="ident")
 
-        nc.vector.memset(xt_sc[:].rearrange("p z c -> p (z c)").bitcast(I32), 0)
-        nc.vector.memset(wa_sc[:].rearrange("p z c -> p (z c)").bitcast(I32), 0)
-        nc.gpsimd.memset(wb_sc[:].rearrange("p z c -> p (z c)").bitcast(I32), 0)
-        load_scale_rows(nc.gpsimd, wb_sc, wb_scales)
+        for plane in (xt_sc, wb_sc, wa_sc):
+            nc.vector.memset(plane[:].rearrange("p z c -> p (z c)").bitcast(I32), 0)
+        nc.gpsimd.dma_start(out=bcol[:], in_=bi.rearrange("o (p c) -> p (o c)", c=2))
+
+        ones = sb.tile([P, P], F32, name="ones")
+        ramp = sb.tile([P, P], F32, name="ramp", align_bytes=64)
+        turned = sb.tile([P, P], F32, name="turned", align_bytes=64)
+        dist = sb.tile([P, P], F32, name="dist")
+        nc.vector.memset(ones[:], 1.0)
+        nc.vector.tensor_tensor_scan(ramp[:], ones[:], ones[:], 0.0, ALU.mult, ALU.add)
+        nc.vector.transpose(turned[:], ramp[:])
+        for q in range(0, P, 32):
+            nc.scalar.activation(dist[q : q + 32, :], ramp[q : q + 32, :], ACT.Abs, bias=turned[q : q + 32, q : q + 1], scale=-1.0)
+        nc.scalar.activation(ident[:], dist[:], ACT.Relu, bias=1.0, scale=-1.0)
 
         planes = xs.rearrange("(p u t) s -> u p t s", u=2, t=2)
-        for u in range(2):
-            nc.scalar.dma_start(out=xs_pl[u][:], in_=planes[u])
-        nc.scalar.dma_start(out=xt_w[0][:].bitcast(I32), in_=words_of(xt_words, 0))
-
         nc.sync.dma_start(idx2[:], offs2)
+        nc.sync.dma_start(out=xs_pl[0][:], in_=planes[0])
         nc.sync.dma_start(idx[:], offs)
         load_scale_rows(nc.sync, xt_sc, xt_scales)
+        nc.sync.dma_start(out=xs_pl[1][:], in_=planes[1])
+        nc.sync.dma_start(out=xt_w[0][:].bitcast(I32), in_=words_of(xt_words, 0))
+        load_scale_rows(nc.sync, wb_sc, wb_scales)
         nc.sync.dma_start(out=wb_w[:].bitcast(I32), in_=words_of(wb_words, 0))
-        nc.sync.dma_start(out=bcol[:], in_=bi.rearrange("o (j c) -> o j c", c=8).broadcast_to([4, 32, 8]))
         nc.sync.dma_start(out=xt_w[1][:].bitcast(I32), in_=words_of(xt_words, 1))
         nc.sync.dma_start(out=wa_w[:].bitcast(I32), in_=wa_words.rearrange("z p c r -> p z (c r)").bitcast(I32))
         load_scale_rows(nc.sync, wa_sc, wa_scales)
@@ -77,26 +87,27 @@ def tile_list_rows_othertable_gapoverpeak_kernel(
         for z in range(PASSES):
             nc.vector.tensor_copy(xt_gs[:, z, :], xt_sc[:, z, :].indirect(idx[:]))
 
-        spread = sb.tile([P, 8, 32], F32, name="spread", align_bytes=64)
-        turned = sb.tile([P, 8, 32], F32, name="turned", align_bytes=64)
-        nc.vector.tensor_copy(spread[:], bcol[:].unsqueeze(2).broadcast_to([P, 8, 32]))
-        nc.vector.transpose(turned[:].rearrange("p c j -> p (c j)"), spread[:].rearrange("p c j -> p (c j)"))
-
-        picked = sb.tile([P, PACK, J], F32, name="picked", align_bytes=64)
-        for t in range(PACK):
+        picked = sb.tile([P, PACK, J], F32, name="picked", tag="xt_g0", align_bytes=64)
+        for t in range(PACK - 1):
             nc.scalar.activation(picked[:, t, :], xs_pl[t // 2][:, t % 2, :].indirect(idx2[:]), COPY)
-        woven = sb.tile([P, J, PACK], BF16, name="woven", tag="reused", align_bytes=64)
-        nc.vector.tensor_scalar(woven[:], picked[:].rearrange("p t c -> p c t"), -1.0, None, ALU.mult)
+        nc.vector.tensor_copy(picked[:, PACK - 1, :], xs_pl[1][:, 1, :].indirect(idx2[:]))
+        woven = sb.tile([P, J, PACK], BF16, name="woven", align_bytes=64)
+        nc.vector.tensor_scalar(
+            woven[:].rearrange("p (c i) t -> p c t i", i=4), picked[:].rearrange("p t (c i) -> p c t i", i=4), -1.0, None, ALU.mult
+        )
         xs_q = sb.tile([P, J], U32, name="xs_q", align_bytes=64)
         xs_qs = sb.tile([P, J], U8, name="xs_qs", align_bytes=64)
         nc.vector.quantize_mx(out=xs_q[:].bitcast(E5M2X4), scales=xs_qs[:], in_=woven[:].rearrange("p c t -> p (c t)"))
 
-        xt_g = [sb.tile([P, J], U32, name=f"xt_g{z}", align_bytes=64) for z in range(PASSES)]
+        xt_g = [sb.tile([P, J], U32, name=f"xt_g{z}", tag=f"xt_g{z}", align_bytes=64) for z in range(PASSES)]
         for z in range(PASSES):
             nc.vector.tensor_copy(xt_g[z][:], xt_w[z][:].indirect(idx[:]))
 
-        bias = sb.tile([P, 32, 8], F32, name="bias")
-        nc.scalar.copy(bias[:], turned[:].rearrange("p c j -> p j c"))
+        bias_ps = ps.tile([P, 2, P], F32, name="bias_ps")
+        for c in range(2):
+            nc.tensor.transpose(bias_ps[:, c, :], bcol[:, c : c + 1].to_broadcast([P, P]), ident[:])
+        bias = sb.tile([P, P, 2], F32, name="bias", tag="xs_pl1", align_bytes=64)
+        nc.scalar.copy(bias[:], bias_ps[:].rearrange("p c m -> p m c"))
 
         acc = [ps.tile([P, N], F32, name=f"acc{h}") for h in range(TILES)]
         for h in range(TILES):
@@ -117,17 +128,24 @@ def tile_list_rows_othertable_gapoverpeak_kernel(
         nc.scalar.activation(res3[:], res[:], COPY, scale=0.3)
 
         gap = [sb.tile([P, N], F32, name=f"gap{h}") for h in range(TILES)]
-        peak = sb.tile([P, TILES], F32, name="peak")
-        den = sb.tile([P, TILES], F32, name="den")
-        inv = sb.tile([P, TILES], F32, name="inv")
-        for h in range(TILES):
-            nc.vector.tensor_tensor(gap[h][:], acc[h][:], bias[:].rearrange("p j c -> p (j c)"), ALU.subtract)
-        for h in range(TILES):
-            nc.vector.tensor_reduce(peak[:, h : h + 1], gap[h][:], mybir.AxisListType.X, ALU.max, apply_absolute_value=True)
-        nc.vector.tensor_scalar(den[:], peak[:], 0.2, None, ALU.add)
-        nc.vector.reciprocal(inv[:], den[:])
-        stores = (nc.sync, nc.scalar)
-        for h in range(TILES):
+        inv = [sb.tile([P, 1], F32, name=f"inv{h}") for h in range(TILES)]
+
+        def measure(h):
+            peak = sb.tile([P, 1], F32, name=f"peak{h}")
+            den = sb.tile([P, 1], F32, name=f"den{h}")
+            nc.vector.tensor_reduce(peak[:], gap[h][:], mybir.AxisListType.X, ALU.max, apply_absolute_value=True)
+            nc.vector.tensor_scalar(den[:], peak[:], 0.2, None, ALU.add)
+            nc.vector.reciprocal(inv[h][:], den[:])
+
+        def finish(h, queue):
             y = sb.tile([P, N], F32, name=f"y{h}")
-            nc.vector.scalar_tensor_tensor(y[:], gap[h][:], inv[:, h : h + 1], res3[:, h, :], ALU.mult, ALU.add)
-            stores[h].dma_start(out=out[h * P : (h + 1) * P, :], in_=y[:])
+            nc.vector.scalar_tensor_tensor(y[:], gap[h][:], inv[h][:], res3[:, h, :], ALU.mult, ALU.add)
+            queue.dma_start(out=out[h * P : (h + 1) * P, :], in_=y[:])
+
+        bias_row = bias[:].rearrange("p m c -> p (m c)")
+        nc.vector.tensor_tensor(gap[0][:], acc[0][:], bias_row, ALU.subtract)
+        measure(0)
+        nc.vector.tensor_tensor(gap[1][:], acc[1][:], bias_row, ALU.subtract)
+        finish(0, nc.scalar)
+        measure(1)
+        finish(1, nc.sync)

@@ -23,9 +23,9 @@ PASSES = K // (P * PACK)
 TILES = J // P
 
 
-def load_scale_rows(queue, plane, scales):
+def load_scale_rows(queue, plane, scales, which=range(4)):
     rows = scales.bitcast(I32).rearrange("z (q r) c -> r q z c", r=4)
-    for r in range(4):
+    for r in which:
         queue.dma_start(out=plane[r:P:32, :, :].bitcast(I32), in_=rows[r])
 
 
@@ -71,15 +71,16 @@ def tile_list_rows_othertable_gapoverpeak_kernel(
 
         planes = xs.rearrange("(p u t) s -> u p t s", u=2, t=2)
         nc.sync.dma_start(idx2[:], offs2)
-        nc.sync.dma_start(out=xs_pl[0][:], in_=planes[0])
         nc.sync.dma_start(idx[:], offs)
+        nc.sync.dma_start(out=xs_pl[0][:], in_=planes[0])
         load_scale_rows(nc.sync, xt_sc, xt_scales)
         nc.sync.dma_start(out=xs_pl[1][:], in_=planes[1])
-        nc.sync.dma_start(out=xt_w[0][:].bitcast(I32), in_=words_of(xt_words, 0))
-        load_scale_rows(nc.sync, wb_sc, wb_scales)
         nc.sync.dma_start(out=wb_w[:].bitcast(I32), in_=words_of(wb_words, 0))
-        nc.sync.dma_start(out=xt_w[1][:].bitcast(I32), in_=words_of(xt_words, 1))
         nc.sync.dma_start(out=wa_w[:].bitcast(I32), in_=wa_words.rearrange("z p c r -> p z (c r)").bitcast(I32))
+        load_scale_rows(nc.sync, wb_sc, wb_scales, range(0, 2))
+        nc.sync.dma_start(out=xt_w[0][:].bitcast(I32), in_=words_of(xt_words, 0))
+        load_scale_rows(nc.sync, wb_sc, wb_scales, range(2, 4))
+        nc.sync.dma_start(out=xt_w[1][:].bitcast(I32), in_=words_of(xt_words, 1))
         load_scale_rows(nc.sync, wa_sc, wa_scales)
         nc.sync.dma_start(out=res[:], in_=rs.rearrange("(h p) n -> p h n", p=P))
 
@@ -87,21 +88,24 @@ def tile_list_rows_othertable_gapoverpeak_kernel(
         for z in range(PASSES):
             nc.vector.tensor_copy(xt_gs[:, z, :], xt_sc[:, z, :].indirect(idx[:]))
 
-        picked = sb.tile([P, PACK, J], F32, name="picked", tag="xt_g0", align_bytes=64)
+        picked = sb.tile([P, PACK, J], F32, name="picked", align_bytes=64)
         for t in range(PACK - 1):
             nc.scalar.activation(picked[:, t, :], xs_pl[t // 2][:, t % 2, :].indirect(idx2[:]), COPY)
         nc.vector.tensor_copy(picked[:, PACK - 1, :], xs_pl[1][:, 1, :].indirect(idx2[:]))
         woven = sb.tile([P, J, PACK], BF16, name="woven", align_bytes=64)
-        nc.vector.tensor_scalar(
-            woven[:].rearrange("p (c i) t -> p c t i", i=4), picked[:].rearrange("p t (c i) -> p c t i", i=4), -1.0, None, ALU.mult
-        )
+        dst = woven[:].rearrange("p (c i) t -> p c t i", i=4)
+        src = picked[:].rearrange("p t (c i) -> p c t i", i=4)
+        split = 36
+        nc.vector.tensor_scalar(dst[:, :split], src[:, :split], -1.0, None, ALU.mult)
+        nc.scalar.activation(dst[:, split:], src[:, split:], COPY, scale=-1.0)
         xs_q = sb.tile([P, J], U32, name="xs_q", align_bytes=64)
         xs_qs = sb.tile([P, J], U8, name="xs_qs", align_bytes=64)
         nc.vector.quantize_mx(out=xs_q[:].bitcast(E5M2X4), scales=xs_qs[:], in_=woven[:].rearrange("p c t -> p (c t)"))
 
-        xt_g = [sb.tile([P, J], U32, name=f"xt_g{z}", tag=f"xt_g{z}", align_bytes=64) for z in range(PASSES)]
-        for z in range(PASSES):
-            nc.vector.tensor_copy(xt_g[z][:], xt_w[z][:].indirect(idx[:]))
+        xt_g = [sb.tile([P, J], U32, name=f"xt_g{z}", align_bytes=64) for z in range(PASSES)]
+        nc.vector.tensor_copy(xt_g[0][:], xt_w[0][:].indirect(idx[:]))
+        for h in range(TILES):
+            nc.vector.tensor_copy(xt_g[1][:, h * P : (h + 1) * P], xt_w[1][:].indirect(idx[:, h * P // 16 : (h + 1) * P // 16]))
 
         bias_ps = ps.tile([P, 2, P], F32, name="bias_ps")
         for c in range(2):
@@ -110,42 +114,37 @@ def tile_list_rows_othertable_gapoverpeak_kernel(
         nc.scalar.copy(bias[:], bias_ps[:].rearrange("p c m -> p m c"))
 
         acc = [ps.tile([P, N], F32, name=f"acc{h}") for h in range(TILES)]
-        for h in range(TILES):
-            cols = slice(h * P, (h + 1) * P)
-            nc.tensor.matmul_mx(
-                out=acc[h][:], lhsT=xs_q[:, cols].bitcast(E5M2X4), lhsT_scale=xs_qs[:, cols],
-                rhs=wb_w[:].bitcast(E4M3X4), rhs_scale=wb_sc[:, 0, :], start=True, stop=False,
-            )
-        for h in range(TILES):
-            cols = slice(h * P, (h + 1) * P)
-            for z in range(PASSES):
+        passes = [
+            (xs_q, xs_qs[:], wb_w[:].bitcast(E4M3X4), wb_sc[:, 0, :]),
+            (xt_g[0], xt_gs[:, 0, :], wa_w[:, 0, :].bitcast(E5M2X4), wa_sc[:, 0, :]),
+            (xt_g[1], xt_gs[:, 1, :], wa_w[:, 1, :].bitcast(E5M2X4), wa_sc[:, 1, :]),
+        ]
+        for i, (codes, scales, w_codes, w_scales) in enumerate(passes):
+            for h in range(TILES):
+                cols = slice(h * P, (h + 1) * P)
                 nc.tensor.matmul_mx(
-                    out=acc[h][:], lhsT=xt_g[z][:, cols].bitcast(E5M2X4), lhsT_scale=xt_gs[:, z, cols],
-                    rhs=wa_w[:, z, :].bitcast(E5M2X4), rhs_scale=wa_sc[:, z, :], start=False, stop=(z == PASSES - 1),
+                    out=acc[h][:], lhsT=codes[:, cols].bitcast(E5M2X4), lhsT_scale=scales[:, cols],
+                    rhs=w_codes, rhs_scale=w_scales, start=(i == 0), stop=(i == len(passes) - 1),
                 )
 
         res3 = sb.tile([P, TILES, N], F32, name="res3")
         nc.scalar.activation(res3[:], res[:], COPY, scale=0.3)
 
-        gap = [sb.tile([P, N], F32, name=f"gap{h}") for h in range(TILES)]
-        inv = [sb.tile([P, 1], F32, name=f"inv{h}") for h in range(TILES)]
-
-        def measure(h):
-            peak = sb.tile([P, 1], F32, name=f"peak{h}")
-            den = sb.tile([P, 1], F32, name=f"den{h}")
-            nc.vector.tensor_reduce(peak[:], gap[h][:], mybir.AxisListType.X, ALU.max, apply_absolute_value=True)
-            nc.vector.tensor_scalar(den[:], peak[:], 0.2, None, ALU.add)
-            nc.vector.reciprocal(inv[h][:], den[:])
-
-        def finish(h, queue):
-            y = sb.tile([P, N], F32, name=f"y{h}")
-            nc.vector.scalar_tensor_tensor(y[:], gap[h][:], inv[h][:], res3[:, h, :], ALU.mult, ALU.add)
-            queue.dma_start(out=out[h * P : (h + 1) * P, :], in_=y[:])
-
         bias_row = bias[:].rearrange("p m c -> p (m c)")
-        nc.vector.tensor_tensor(gap[0][:], acc[0][:], bias_row, ALU.subtract)
-        measure(0)
-        nc.vector.tensor_tensor(gap[1][:], acc[1][:], bias_row, ALU.subtract)
-        finish(0, nc.scalar)
-        measure(1)
-        finish(1, nc.sync)
+        gap = [sb.tile([P, N], F32, name=f"gap{h}") for h in range(TILES)]
+        peak = [sb.tile([P, 1], F32, name=f"peak{h}") for h in range(TILES)]
+        den = [sb.tile([P, 1], F32, name=f"den{h}") for h in range(TILES)]
+        inv = [sb.tile([P, 1], F32, name=f"inv{h}") for h in range(TILES)]
+        for h in range(TILES):
+            nc.vector.tensor_tensor(gap[h][:], acc[h][:], bias_row, ALU.subtract)
+        for h in range(TILES):
+            nc.vector.tensor_reduce(peak[h][:], gap[h][:], mybir.AxisListType.X, ALU.max, apply_absolute_value=True)
+        for h in range(TILES):
+            nc.vector.tensor_scalar(den[h][:], peak[h][:], 0.2, None, ALU.add)
+        for h in range(TILES):
+            nc.vector.reciprocal(inv[h][:], den[h][:])
+        pieces = [(0, slice(0, N), nc.scalar), (1, slice(0, N // 2), nc.sync), (1, slice(N // 2, N), nc.scalar)]
+        for i, (h, cols, queue) in enumerate(pieces):
+            y = sb.tile([P, cols.stop - cols.start], F32, name=f"y{i}")
+            nc.vector.scalar_tensor_tensor(y[:], gap[h][:, cols], inv[h][:], res3[:, h, cols], ALU.mult, ALU.add)
+            queue.dma_start(out=out[h * P : (h + 1) * P, cols], in_=y[:])

from contextlib import ExitStack

import concourse.mybir as mybir

K, T, J, N, S, L = 1024, 1024, 256, 256, 512, 512
FLOPS = 2 * J * N * (K + L)

F32 = mybir.dt.float32
BF16 = mybir.dt.bfloat16
I32 = mybir.dt.int32
U32 = mybir.dt.uint32
U16 = mybir.dt.uint16
U8 = mybir.dt.uint8
E5M2X4 = mybir.dt.float8_e5m2_x4
E4M3X4 = mybir.dt.float8_e4m3fn_x4
ALU = mybir.AluOpType
ACT = mybir.ActivationFunctionType
COPY = ACT.Copy

P = 128
PACK = 4
PASSES = K // (P * PACK)
TILES = J // P


def load_scale_rows(queue, plane, scales, which=range(4)):
    rows = scales.bitcast(I32).rearrange("z (q r) c -> r q z c", r=4)
    for r in which:
        queue.dma_start(out=plane[r:P:32, :, :].bitcast(I32), in_=rows[r])


def words_of(packed, z):
    return packed[z].rearrange("p c r -> p (c r)").bitcast(I32)


def tile_list_rows_othertable_gapoverpeak_kernel(
    tc, xt_words, xt_scales, wa_words, wa_scales, xs, wb_words, wb_scales, bi, rs, offs, offs2, out
):
    nc = tc.nc
    with ExitStack() as ctx:
        sb = ctx.enter_context(tc.tile_pool(name="sb", bufs=1))
        ps = ctx.enter_context(tc.psum_pool(name="ps", bufs=1))

        idx = sb.tile([P, J // 16], U16, name="idx")
        idx2 = sb.tile([P, J // 16], U16, name="idx2")
        xt_sc = sb.tile([P, PASSES, T], U8, name="xt_sc", align_bytes=64)
        wa_sc = sb.tile([P, PASSES, N], U8, name="wa_sc", align_bytes=64)
        wb_sc = sb.tile([P, 1, N], U8, name="wb_sc", align_bytes=64)
        xs_pl = [sb.tile([P, 2, S], F32, name=f"xs_pl{u}", tag=f"xs_pl{u}", align_bytes=64) for u in range(2)]
        xt_w = [sb.tile([P, T], U32, name=f"xt_w{z}", align_bytes=64) for z in range(PASSES)]
        wa_w = sb.tile([P, PASSES, N], U32, name="wa_w", align_bytes=64)
        wb_w = sb.tile([P, N], U32, name="wb_w", align_bytes=64)
        bcol = sb.tile([P, 2], F32, name="bcol")
        res = sb.tile([P, TILES, N], F32, name="res")
        ident = sb.tile([P, P], F32, name="ident")

        for plane in (xt_sc, wb_sc, wa_sc):
            nc.vector.memset(plane[:].rearrange("p z c -> p (z c)").bitcast(I32), 0)
        nc.gpsimd.dma_start(out=bcol[:], in_=bi.rearrange("o (p c) -> p (o c)", c=2))

        ones = sb.tile([P, P], F32, name="ones")
        ramp = sb.tile([P, P], F32, name="ramp", align_bytes=64)
        turned = sb.tile([P, P], F32, name="turned", align_bytes=64)
        dist = sb.tile([P, P], F32, name="dist")
        nc.vector.memset(ones[:], 1.0)
        nc.vector.tensor_tensor_scan(ramp[:], ones[:], ones[:], 0.0, ALU.mult, ALU.add)
        nc.vector.transpose(turned[:], ramp[:])
        for q in range(0, P, 32):
            nc.scalar.activation(dist[q : q + 32, :], ramp[q : q + 32, :], ACT.Abs, bias=turned[q : q + 32, q : q + 1], scale=-1.0)
        nc.scalar.activation(ident[:], dist[:], ACT.Relu, bias=1.0, scale=-1.0)

        planes = xs.rearrange("(p u t) s -> u p t s", u=2, t=2)
        nc.sync.dma_start(idx2[:], offs2)
        nc.sync.dma_start(idx[:], offs)
        nc.sync.dma_start(out=xs_pl[0][:], in_=planes[0])
        load_scale_rows(nc.sync, xt_sc, xt_scales)
        nc.sync.dma_start(out=xs_pl[1][:], in_=planes[1])
        nc.sync.dma_start(out=wb_w[:].bitcast(I32), in_=words_of(wb_words, 0))
        nc.sync.dma_start(out=wa_w[:].bitcast(I32), in_=wa_words.rearrange("z p c r -> p z (c r)").bitcast(I32))
        load_scale_rows(nc.sync, wb_sc, wb_scales, range(0, 2))
        nc.sync.dma_start(out=xt_w[0][:].bitcast(I32), in_=words_of(xt_words, 0))
        load_scale_rows(nc.sync, wb_sc, wb_scales, range(2, 4))
        nc.sync.dma_start(out=xt_w[1][:].bitcast(I32), in_=words_of(xt_words, 1))
        load_scale_rows(nc.sync, wa_sc, wa_scales)
        nc.sync.dma_start(out=res[:], in_=rs.rearrange("(h p) n -> p h n", p=P))

        xt_gs = sb.tile([P, PASSES, J], U8, name="xt_gs", align_bytes=64)
        for z in range(PASSES):
            nc.vector.tensor_copy(xt_gs[:, z, :], xt_sc[:, z, :].indirect(idx[:]))

        picked = sb.tile([P, PACK, J], F32, name="picked", align_bytes=64)
        for t in range(PACK - 1):
            nc.scalar.activation(picked[:, t, :], xs_pl[t // 2][:, t % 2, :].indirect(idx2[:]), COPY)
        nc.vector.tensor_copy(picked[:, PACK - 1, :], xs_pl[1][:, 1, :].indirect(idx2[:]))
        woven = sb.tile([P, J, PACK], BF16, name="woven", align_bytes=64)
        dst = woven[:].rearrange("p (c i) t -> p c t i", i=4)
        src = picked[:].rearrange("p t (c i) -> p c t i", i=4)
        split = 36
        nc.vector.tensor_scalar(dst[:, :split], src[:, :split], -1.0, None, ALU.mult)
        nc.scalar.activation(dst[:, split:], src[:, split:], COPY, scale=-1.0)
        xs_q = sb.tile([P, J], U32, name="xs_q", align_bytes=64)
        xs_qs = sb.tile([P, J], U8, name="xs_qs", align_bytes=64)
        nc.vector.quantize_mx(out=xs_q[:].bitcast(E5M2X4), scales=xs_qs[:], in_=woven[:].rearrange("p c t -> p (c t)"))

        xt_g = [sb.tile([P, J], U32, name=f"xt_g{z}", align_bytes=64) for z in range(PASSES)]
        nc.vector.tensor_copy(xt_g[0][:], xt_w[0][:].indirect(idx[:]))
        for h in range(TILES):
            nc.vector.tensor_copy(xt_g[1][:, h * P : (h + 1) * P], xt_w[1][:].indirect(idx[:, h * P // 16 : (h + 1) * P // 16]))

        bias_ps = ps.tile([P, 2, P], F32, name="bias_ps")
        for c in range(2):
            nc.tensor.transpose(bias_ps[:, c, :], bcol[:, c : c + 1].to_broadcast([P, P]), ident[:])
        bias = sb.tile([P, P, 2], F32, name="bias", tag="xs_pl1", align_bytes=64)
        nc.scalar.copy(bias[:], bias_ps[:].rearrange("p c m -> p m c"))

        acc = [ps.tile([P, N], F32, name=f"acc{h}") for h in range(TILES)]
        passes = [
            (xs_q, xs_qs[:], wb_w[:].bitcast(E4M3X4), wb_sc[:, 0, :]),
            (xt_g[0], xt_gs[:, 0, :], wa_w[:, 0, :].bitcast(E5M2X4), wa_sc[:, 0, :]),
            (xt_g[1], xt_gs[:, 1, :], wa_w[:, 1, :].bitcast(E5M2X4), wa_sc[:, 1, :]),
        ]
        for i, (codes, scales, w_codes, w_scales) in enumerate(passes):
            for h in range(TILES):
                cols = slice(h * P, (h + 1) * P)
                nc.tensor.matmul_mx(
                    out=acc[h][:], lhsT=codes[:, cols].bitcast(E5M2X4), lhsT_scale=scales[:, cols],
                    rhs=w_codes, rhs_scale=w_scales, start=(i == 0), stop=(i == len(passes) - 1),
                )

        res3 = sb.tile([P, TILES, N], F32, name="res3")
        nc.scalar.activation(res3[:], res[:], COPY, scale=0.3)

        bias_row = bias[:].rearrange("p m c -> p (m c)")
        gap = [sb.tile([P, N], F32, name=f"gap{h}") for h in range(TILES)]
        peak = [sb.tile([P, 1], F32, name=f"peak{h}") for h in range(TILES)]
        den = [sb.tile([P, 1], F32, name=f"den{h}") for h in range(TILES)]
        inv = [sb.tile([P, 1], F32, name=f"inv{h}") for h in range(TILES)]
        for h in range(TILES):
            nc.vector.tensor_tensor(gap[h][:], acc[h][:], bias_row, ALU.subtract)
        for h in range(TILES):
            nc.vector.tensor_reduce(peak[h][:], gap[h][:], mybir.AxisListType.X, ALU.max, apply_absolute_value=True)
        for h in range(TILES):
            nc.vector.tensor_scalar(den[h][:], peak[h][:], 0.2, None, ALU.add)
        for h in range(TILES):
            nc.vector.reciprocal(inv[h][:], den[h][:])
        pieces = [(0, slice(0, N), nc.scalar), (1, slice(0, N // 2), nc.sync), (1, slice(N // 2, N), nc.scalar)]
        for i, (h, cols, queue) in enumerate(pieces):
            y = sb.tile([P, cols.stop - cols.start], F32, name=f"y{i}")
            nc.vector.scalar_tensor_tensor(y[:], gap[h][:, cols], inv[h][:], res3[:, h, cols], ALU.mult, ALU.add)
            queue.dma_start(out=out[h * P : (h + 1) * P, cols], in_=y[:])
